import numpy as np
import ml_dtypes


def mxq(x, axis, fmt="e4m3"):
    dtype, down = {"e4m3": (ml_dtypes.float8_e4m3fn, 7), "e5m2": (ml_dtypes.float8_e5m2, 14)}[fmt]
    v = np.moveaxis(np.asarray(x, np.float32).astype(ml_dtypes.bfloat16).astype(np.float64), axis, -1)
    blocks = v.reshape(v.shape[:-1] + (-1, 32))
    amax = np.abs(blocks).max(-1, keepdims=True)
    byte = np.maximum(np.where(amax > 0, np.frexp(amax)[1] - 1 + 127, 0) - down, 1)
    scale = np.exp2(byte - 127.0)
    codes = (blocks / scale).astype(np.float32).astype(dtype).astype(np.float64)
    return np.moveaxis((codes * scale).reshape(v.shape), -1, axis)


WIDE = False


def mx_kscale(k):
    if not WIDE:
        return np.ones(k)
    levels = np.array([10, -10, 5, -5, 0])
    if k % 512:
        return np.exp2(np.random.permutation(np.resize(levels, k // 32))).repeat(32)
    a = np.empty((k // 512, 16))
    for p in range(k // 512):
        a[p, :8] = np.random.permutation(np.resize(levels, 8))
        for g in range(8):
            far = levels[np.abs(levels - a[p, g]) >= 10]
            a[p, g + 8] = far[np.random.randint(len(far))]
    return np.exp2(a.ravel()).repeat(32)


def f64(x):
    return np.asarray(x).astype(np.float64)


def striped(idx):
    return np.tile(idx.reshape(-1, 16).T, (8, 1)).astype(np.uint16)


def unstriped(offs):
    return offs[:16].T.reshape(-1).astype(np.int64)


E2M1 = np.array([0.0, 0.5, 1.0, 1.5, 2.0, 3.0, 4.0, 6.0, -0.0, -0.5, -1.0, -1.5, -2.0, -3.0, -4.0, -6.0])


def pack_weight(w, fmt):
    k, n = w.shape
    w = f64(np.asarray(w, np.float32).astype(ml_dtypes.bfloat16)).reshape(k // 32, 32, n)
    amax = np.abs(w).max(1)
    if fmt == "e4m3":
        byte = np.frexp(amax)[1] - 1 + 127 - 7
    else:
        mant, ex = np.frexp(amax / 6.0)
        byte = np.where(mant > 0.5, ex, ex - 1) + 127
    byte = np.clip(np.where(amax > 0, byte, 1), 1, 254)
    scaled = (w * np.exp2(127.0 - byte)[:, None, :]).reshape(k, n).astype(np.float32)
    by_word = np.ascontiguousarray(scaled.reshape(k // 512, 128, 4, n).transpose(0, 1, 3, 2))
    if fmt == "e4m3":
        words = by_word.astype(ml_dtypes.float8_e4m3fn).view(np.uint8)
    else:
        c = by_word.astype(ml_dtypes.float4_e2m1fn).view(np.uint8) & 0xF
        words = (c[..., 0::2] | (c[..., 1::2] << 4)).reshape(k // 512, 128, 2 * n)
    return np.ascontiguousarray(words), np.ascontiguousarray(byte.astype(np.uint8).reshape(k // 512, 16, n))


def unpack_weight(words, scales, fmt):
    g, _, n = scales.shape
    words = np.ascontiguousarray(words).reshape(g, 128, n, -1)
    if fmt == "e4m3":
        vals = words.view(ml_dtypes.float8_e4m3fn).astype(np.float64)
    else:
        nib = np.empty((g, 128, n, 4), np.uint8)
        nib[..., 0::2] = words & 0xF
        nib[..., 1::2] = words >> 4
        vals = E2M1[nib]
    vals = vals * np.repeat(np.exp2(scales.astype(np.float64) - 127.0), 8, axis=1)[..., None]
    return vals.transpose(0, 1, 3, 2).reshape(g * 512, n)


def gelu(v):
    return 0.5 * v * (1.0 + np.tanh(np.sqrt(2.0 / np.pi) * (v + 0.044715 * v**3)))


K, T, S, H, T2, P = 512, 2048, 512, 1024, 1024, 512

def setup_inputs():
    n = np.random.standard_normal
    s = mx_kscale(K)[:, None]
    u = mx_kscale(H)[:, None]
    d = {}
    d["tab_words"], d["tab_scales"] = pack_weight(n((K, T)) * s, "e4m3")
    d["offs"] = striped(np.random.permutation(T)[:S])
    d["wa"] = (0.4 * n((K, H)) / s / K ** 0.5).astype(np.float32)
    d["wb_words"], d["wb_scales"] = pack_weight(0.56 * n((K, H)) / s / K ** 0.5, "e2m1")
    d["gain"] = (np.exp(0.3 * n(H)) * u[:, 0]).astype(np.float32)
    d["page0"] = (n((H, T2)) * u).astype(np.float32)
    d["wgs"] = np.exp(0.3 * n((128, S))).astype(np.float32)
    d["offs2"] = striped(np.random.permutation(T2)[:S])
    d["offs3"] = striped(np.random.permutation(T2)[:P])
    d["offs4"] = striped(np.random.permutation(T2)[:P])
    d["sc"] = np.exp(0.4 * n(H)).astype(np.float32)
    d["w2"] = (n((H, H)) / u / H ** 0.5).astype(np.float32)
    d["w3_words"], d["w3_scales"] = pack_weight(1.4 * n((H, H)) / u / H ** 0.5, "e4m3")
    d["wv"] = (0.8 * np.exp(0.3 * n(H)) / u[:, 0]).astype(np.float32)
    return d

def reference(tab_words, tab_scales, offs, wa, wb_words, wb_scales, gain, page0, wgs, offs2, offs3, offs4, sc, w2, w3_words, w3_scales, wv):
    v = unpack_weight(tab_words, tab_scales, "e4m3")[:, unstriped(offs)]
    wb = unpack_weight(wb_words, wb_scales, "e2m1")
    w3 = unpack_weight(w3_words, w3_scales, "e4m3")
    lin = mxq(f64(wa), 0, "e4m3").T @ v
    ang = wb.T @ v
    h = (lin + np.cos(ang)) * f64(gain)[:, None]
    page = f64(page0).copy()
    page[:, unstriped(offs2)] = np.tile(f64(wgs), (H // 128, 1)) * h
    x = page[:, unstriped(offs3)]
    xs = x * f64(sc)[:, None]
    b = np.tanh(mxq(f64(w2), 0, "e4m3").T @ mxq(xs, 0, "e4m3"))
    t = b * x
    y = w3.T @ mxq(t, 0, "e4m3")
    return y + page[:, unstriped(offs4)] * f64(wv)[:, None]

@@ -1,0 +1,330 @@
+import math
+from contextlib import ExitStack
+
+import concourse.mybir as mybir
+from concourse.masks import make_identity
+
+K, T, S, H, T2, NP = 512, 2048, 512, 1024, 1024, 512
+FLOPS = 2 * (2 * K * H * S + 2 * H * H * NP)
+
+F32 = mybir.dt.float32
+BF16 = mybir.dt.bfloat16
+I32 = mybir.dt.int32
+U32 = mybir.dt.uint32
+U16 = mybir.dt.uint16
+U8 = mybir.dt.uint8
+FP8X4 = mybir.dt.float8_e4m3fn_x4
+FP4X4 = mybir.dt.float4_e2m1fn_x4
+ACT = mybir.ActivationFunctionType
+ALU = mybir.AluOpType
+
+P = 128
+PACK = 4
+BLOCK = P * PACK
+NBLK = H // BLOCK
+NSLICE = H // P
+ROUNDER = 1.5 * 2.0**23
+
+
+def tile_list_division_member_page_kernel(
+    tc, tab_words, tab_scales, offs, wa, wb_words, wb_scales, gain, page0, wgs, offs2, offs3, offs4, sc, w2,
+    w3_words, w3_scales, wv, out,
+):
+    nc = tc.nc
+    with ExitStack() as ctx:
+        keep = ctx.enter_context(tc.tile_pool(name="keep", bufs=1))
+        ring = ctx.enter_context(tc.tile_pool(name="ring", bufs=2))
+        psum = ctx.enter_context(tc.psum_pool(name="psum", bufs=2))
+
+        def kept(shape, dtype, name, tag=None):
+            return keep.tile(shape, dtype, name=name, tag=tag or name, align_bytes=64)
+
+        def load_list(src, name):
+            tile = keep.tile([P, S // 16], U16, name=name)
+            nc.sync.dma_start(tile[:], src)
+            return tile
+
+        def load_scale_rows(queues, plane, src):
+            for quad in range(4):
+                queues[quad].dma_start(
+                    plane[32 * quad : 32 * quad + 4, :].bitcast(I32), src[0, 4 * quad : 4 * quad + 4, :].bitcast(I32)
+                )
+
+        def load_weight_block(w, a, b, name):
+            raw = ring.tile([P, PACK, BLOCK], F32, name=name, tag="raw", bufs=4)
+            rows = w[BLOCK * a : BLOCK * (a + 1), BLOCK * b : BLOCK * (b + 1)]
+            nc.sync.dma_start(raw[:], rows.rearrange("(p i) c -> p i c", i=PACK))
+            return raw
+
+        def load_wb_words(b):
+            raw = kept([P, 2 * BLOCK], U8, "wb_raw%d" % b)
+            nc.sync.dma_start(raw[:].bitcast(I32), wb_words[0, :, 2 * BLOCK * b : 2 * BLOCK * (b + 1)].bitcast(I32))
+            return raw
+
+        def load_page(s):
+            a, i = divmod(s, PACK)
+            page = kept([P, T2], F32, "page%d" % s)
+            rows = page0[BLOCK * a : BLOCK * (a + 1), :].rearrange("(p i) c -> p i c", i=PACK)
+            nc.sync.dma_start(page[:], rows[:, i, :])
+            return page
+
+        def load_vector(vec, name):
+            tile = kept([P, NBLK, PACK], F32, name)
+            nc.gpsimd.dma_start(tile[:], vec.rearrange("(a p i) -> p a i", p=P, i=PACK))
+            return tile
+
+        tab_plane = kept([P, T], U8, "tab_plane")
+        wb_plane_raw = kept([P, H], U8, "wb_plane_raw")
+        w3_plane_raw = kept([P, H], U8, "w3_plane_raw")
+        nc.gpsimd.memset(wb_plane_raw[:].bitcast(I32), 0)
+        nc.gpsimd.memset(tab_plane[:].bitcast(I32), 0)
+        nc.vector.memset(w3_plane_raw[:].bitcast(I32), 0)
+
+        idx = load_list(offs, "idx")
+        wb_raw = [load_wb_words(0)]
+        load_scale_rows([nc.sync] * 4, wb_plane_raw, wb_scales)
+        tab_codes = kept([P, T], I32, "tab_codes")
+        nc.sync.dma_start(tab_codes[:], tab_words[0].rearrange("p t i -> p (t i)").bitcast(I32))
+        load_scale_rows([nc.sync] * 4, tab_plane, tab_scales)
+        ident = kept([P, P], F32, "ident")
+        make_identity(nc, ident[:])
+        gain_t = load_vector(gain, "gain_t")
+        sc_t = load_vector(sc, "sc_t")
+        wv_t = load_vector(wv, "wv_t")
+
+        wa_raw = [load_weight_block(wa, 0, 0, "wa_raw0")]
+        wb_raw.append(load_wb_words(1))
+        pages = [load_page(0)]
+        wgs_t = kept([P, PACK, S], F32, "wgs_t")
+        for quad in range(4):
+            nc.sync.dma_start(wgs_t[32 * quad : 32 * (quad + 1), :, :], wgs.rearrange("(p i) j -> p i j", i=PACK))
+        idx2 = load_list(offs2, "idx2")
+        idx3 = load_list(offs3, "idx3")
+        idx4 = load_list(offs4, "idx4")
+        wa_raw.append(load_weight_block(wa, 0, 1, "wa_raw1"))
+        w2_raw = {}
+        for s in range(1, NSLICE):
+            pages.append(load_page(s))
+            if s % 2 == 1:
+                a, b = divmod(s // 2, NBLK)
+                w2_raw[(a, b)] = load_weight_block(w2, a, b, "w2_raw%d%d" % (a, b))
+        w3_raw = kept([P, NBLK, H], I32, "w3_raw")
+        nc.sync.dma_start(w3_raw[:], w3_words.rearrange("a p n i -> p a (n i)").bitcast(I32))
+        for quad in range(4):
+            nc.sync.dma_start(
+                w3_plane_raw[32 * quad : 32 * quad + 4 * NBLK, :].bitcast(I32),
+                w3_scales[:, 4 * quad : 4 * quad + 4, :].bitcast(I32),
+            )
+
+        v_codes = kept([P, S], U32, "v_codes")
+        v_plane = kept([P, S], U8, "v_plane")
+        wb_codes = kept([P, 2 * H], U8, "wb_codes")
+        wb_plane = kept([P, H], U8, "wb_plane")
+
+        def deal_wb(b):
+            nc.vector.tensor_copy(
+                wb_codes[:].rearrange("p (b i q e) -> p b i q e", b=NBLK, i=PACK, e=2)[:, b],
+                wb_raw[b][:].rearrange("p (q i e) -> p i q e", i=PACK, e=2),
+            )
+            nc.vector.tensor_copy(
+                wb_plane[:].rearrange("p (b i q) -> p b i q", b=NBLK, i=PACK)[:, b],
+                wb_plane_raw[:].rearrange("p (b q i) -> p b i q", b=NBLK, i=PACK)[:, b],
+            )
+
+        def entries(tile, js):
+            return tile[:, js.start // 16 : js.stop // 16]
+
+        halves = [slice(0, S // 2), slice(S // 2, S)]
+        deal_wb(0)
+        for js in halves:
+            nc.vector.tensor_copy(v_codes[:, js], tab_codes[:].bitcast(U32).indirect(entries(idx, js)))
+            nc.vector.tensor_copy(v_plane[:, js], tab_plane[:].indirect(entries(idx, js)))
+
+        def cast_views(raw, grouped, qs):
+            dst = grouped[:].rearrange("p (t q i) -> p q i t", t=PACK, i=PACK)[:, qs]
+            src = raw[:].rearrange("p i (q t) -> p q i t", t=PACK)[:, qs]
+            return dst, src
+
+        def quantise(codes, plane, grouped):
+            nc.vector.quantize_mx(out=codes.bitcast(FP8X4), scales=plane, in_=grouped)
+
+        wa_codes = kept([P, H], U32, "wa_codes")
+        wa_plane = kept([P, H], U8, "wa_plane")
+
+        def prepare_wa(b):
+            grouped = ring.tile([P, PACK * BLOCK], BF16, name="wa_grouped", tag="grouped", align_bytes=64)
+            dst, src = cast_views(wa_raw[b], grouped, slice(0, P))
+            nc.vector.tensor_copy(dst, src)
+            cols = slice(BLOCK * b, BLOCK * (b + 1))
+            quantise(wa_codes[:, cols], wa_plane[:, cols], grouped[:])
+
+        prepare_wa(0)
+
+        def add_transposed(bank, first, second, n):
+            for jt in range(n // P):
+                cols = slice(P * jt, P * (jt + 1))
+                nc.tensor.matmul(bank[:, cols], first[:, cols], ident[:], start=True, stop=False, is_transpose=True)
+                nc.tensor.matmul(bank[:, cols], second[:, cols], ident[:], start=False, stop=True, is_transpose=True)
+
+        x = [kept([P, PACK, NP], F32, "x%d" % a) for a in range(NBLK)]
+        whips = [kept([P, PACK, NP], F32, "whips0")]
+        w2_codes = [kept([P, H], U32, "w2_codes%d" % a) for a in range(NBLK)]
+        w2_plane = [kept([P, H], U8, "w2_plane%d" % a) for a in range(NBLK)]
+        xs_codes = [kept([P, NP], U32, "xs_codes%d" % a) for a in range(NBLK)]
+        xs_plane = [kept([P, NP], U8, "xs_plane%d" % a) for a in range(NBLK)]
+        t_codes = [kept([P, NP], U32, "t_codes%d" % a) for a in range(NBLK)]
+        t_plane = [kept([P, NP], U8, "t_plane%d" % a) for a in range(NBLK)]
+        w2_grouped = {}
+
+        def new_entries(s, js):
+            a, i = divmod(s, PACK)
+            n = js.stop - js.start
+            rows = slice(P * s, P * (s + 1))
+            ang = psum.tile([P, n], F32, name="ang", tag="bank_a")
+            nc.tensor.matmul_mx(
+                out=ang[:], lhsT=wb_codes[:, 2 * P * s : 2 * P * (s + 1)].bitcast(FP4X4), lhsT_scale=wb_plane[:, rows],
+                rhs=v_codes[:, js].bitcast(FP8X4), rhs_scale=v_plane[:, js], start=True, stop=True,
+            )
+            turns = ring.tile([P, n], F32, name="turns")
+            nc.scalar.activation(turns[:], ang[:], ACT.Copy, bias=0.25, scale=1.0 / (2.0 * math.pi))
+            whole = ring.tile([P, n], U32, name="whole")
+            nc.scalar.activation(whole[:], turns[:], ACT.Copy, bias=ROUNDER, scale=1.0)
+            minus = ring.tile([P, n], F32, name="minus")
+            nc.scalar.activation(minus[:], whole[:], ACT.Copy, bias=ROUNDER, scale=-1.0)
+            frac = psum.tile([P, n], F32, name="frac", tag="bank_b")
+            add_transposed(frac, turns, minus, n)
+            lin = psum.tile([P, n], F32, name="lin", tag="bank_c")
+            for jt in range(n // P):
+                cols = slice(js.start + P * jt, js.start + P * (jt + 1))
+                nc.tensor.matmul_mx(
+                    out=lin[:, P * jt : P * (jt + 1)], lhsT=v_codes[:, cols].bitcast(FP8X4), lhsT_scale=v_plane[:, cols],
+                    rhs=wa_codes[:, rows].bitcast(FP8X4), rhs_scale=wa_plane[:, rows], start=True, stop=True,
+                )
+            cos_t = ring.tile([P, n], F32, name="cos_t")
+            nc.scalar.activation(cos_t[:], frac[:], ACT.Sin, scale=2.0 * math.pi)
+            lin_t = ring.tile([P, n], F32, name="lin_t")
+            nc.scalar.copy(lin_t[:], lin[:])
+            total = psum.tile([P, n], F32, name="total", tag="bank_d")
+            add_transposed(total, cos_t, lin_t, n)
+            h = ring.tile([P, n], F32, name="h", bufs=NSLICE)
+            nc.scalar.activation(h[:], total[:], ACT.Copy, scale=gain_t[:, a, i : i + 1])
+            nc.vector.tensor_tensor(pages[s][:].indirect(entries(idx2, js)), h[:], wgs_t[:, i, js], ALU.mult)
+
+        def fetch_x(s):
+            a, i = divmod(s, PACK)
+            nc.vector.tensor_copy(x[a][:, i, :], pages[s][:].indirect(idx3[:]))
+
+        def scale_x(s):
+            a, i = divmod(s, PACK)
+            nc.scalar.activation(xs[a][:, i, :], x[a][:, i, :], ACT.Copy, scale=sc_t[:, a, i : i + 1])
+
+        def fetch_whips(s):
+            a, i = divmod(s, PACK)
+            nc.vector.tensor_copy(whips[a][:, i, :], pages[s][:].indirect(idx4[:]))
+
+        def cast_w2(piece):
+            blk, half = divmod(piece, 2)
+            a, b = divmod(blk, NBLK)
+            if half == 0:
+                w2_grouped[blk] = ring.tile([P, PACK * BLOCK], BF16, name="w2_grouped", tag="grouped", align_bytes=64)
+            dst, src = cast_views(w2_raw[(a, b)], w2_grouped[blk], slice(64 * half, 64 * (half + 1)))
+            nc.scalar.copy(dst, src)
+            if half == 1:
+                cols = slice(BLOCK * b, BLOCK * (b + 1))
+                quantise(w2_codes[a][:, cols], w2_plane[a][:, cols], w2_grouped[blk][:])
+
+        def walk(four_rows):
+            return four_rows.rearrange("p i (c e) -> p c i e", e=4)
+
+        def woven(flat):
+            return flat.rearrange("p (c e i) -> p c i e", e=4, i=PACK)
+
+        def quantise_xs(a, jt):
+            cols = slice(P * jt, P * (jt + 1))
+            xs_woven = ring.tile([P, PACK * P], BF16, name="xs_woven", bufs=3, align_bytes=64)
+            nc.scalar.copy(woven(xs_woven[:]), walk(xs[a][:, :, cols]))
+            quantise(xs_codes[a][:, cols], xs_plane[a][:, cols], xs_woven[:])
+
+        for s in range(NSLICE):
+            for js in halves if s == 0 else [slice(0, S)]:
+                new_entries(s, js)
+            fetch_x(s)
+            if s == 0:
+                deal_wb(1)
+                prepare_wa(1)
+            if s < PACK:
+                fetch_whips(s)
+            if s > 0:
+                cast_w2(s - 1)
+        cast_w2(NSLICE - 1)
+        xs = [kept([P, PACK, NP], BF16, "xs0", "wa_codes"), kept([P, PACK, NP], BF16, "xs1", "wb_codes")]
+        whips.append(kept([P, PACK, NP], F32, "whips1", "wgs_t"))
+        for s in range(PACK):
+            scale_x(s)
+        for jt in range(PACK):
+            quantise_xs(0, jt)
+        for s in range(PACK, NSLICE):
+            scale_x(s)
+
+        w3_codes = kept([P, NBLK, H], I32, "w3_codes")
+        w3_plane = kept([P, H], U8, "w3_plane")
+        nc.vector.tensor_copy(
+            w3_codes[:].rearrange("p a (b i q) -> p (a b) q i", b=NBLK, i=PACK),
+            w3_raw[:].rearrange("p a (b q i) -> p (a b) q i", b=NBLK, i=PACK),
+        )
+        nc.vector.tensor_copy(
+            w3_plane[:].rearrange("p (b i q) -> p b i q", b=NBLK, i=PACK),
+            w3_plane_raw[:].rearrange("p (b q i) -> p b i q", b=NBLK, i=PACK),
+        )
+
+        def second_stage(jt, b):
+            cols = slice(P * jt, P * (jt + 1))
+            bank = psum.tile([P, PACK, P], F32, name="pre_tanh", tag="bank_a" if b == 0 else "bank_b")
+            for i in range(PACK):
+                rows = slice(BLOCK * b + P * i, BLOCK * b + P * (i + 1))
+                for a in range(NBLK):
+                    nc.tensor.matmul_mx(
+                        out=bank[:, i, :], lhsT=w2_codes[a][:, rows].bitcast(FP8X4), lhsT_scale=w2_plane[a][:, rows],
+                        rhs=xs_codes[a][:, cols].bitcast(FP8X4), rhs_scale=xs_plane[a][:, cols],
+                        start=(a == 0), stop=(a == NBLK - 1),
+                    )
+            gate = ring.tile([P, PACK * P], F32, name="gate", bufs=3)
+            gate_walk = gate[:].rearrange("p (c i e) -> p c i e", i=PACK, e=4)
+            nc.scalar.activation(gate_walk, walk(bank[:]), ACT.Tanh)
+            t_woven = ring.tile([P, PACK * P], BF16, name="t_woven", bufs=3, align_bytes=64)
+            nc.vector.tensor_tensor(woven(t_woven[:]), gate_walk, walk(x[b][:, :, cols]), ALU.mult)
+            quantise(t_codes[b][:, cols], t_plane[b][:, cols], t_woven[:])
+
+        def third_stage(half):
+            cols = slice(2 * P * half, 2 * P * (half + 1))
+            for b in range(NBLK):
+                for pair in range(2):
+                    bank = psum.tile([P, 2, 2 * P], F32, name="y", tag="bank_c" if pair == 0 else "bank_d")
+                    res = ring.tile([P, 2, 2 * P], F32, name="res", bufs=4)
+                    for k in range(2):
+                        i = 2 * pair + k
+                        rows = slice(BLOCK * b + P * i, BLOCK * b + P * (i + 1))
+                        for a in range(NBLK):
+                            nc.tensor.matmul_mx(
+                                out=bank[:, k, :], lhsT=w3_codes[:, a, rows].bitcast(FP8X4),
+                                lhsT_scale=w3_plane[4 * a : P, rows],
+                                rhs=t_codes[a][:, cols].bitcast(FP8X4), rhs_scale=t_plane[a][:, cols],
+                                start=(a == 0), stop=(a == NBLK - 1),
+                            )
+                    for k in range(2):
+                        i = 2 * pair + k
+                        nc.vector.scalar_tensor_tensor(
+                            res[:, k, :], whips[b][:, i, cols], wv_t[:, b, i : i + 1], bank[:, k, :], ALU.mult, ALU.add
+                        )
+                    dst = out[BLOCK * b : BLOCK * (b + 1), cols].rearrange("(p i) j -> p i j", i=PACK)
+                    nc.sync.dma_start(dst[:, 2 * pair : 2 * pair + 2, :], res[:])
+
+        for jt in range(PACK):
+            quantise_xs(1, jt)
+            if jt == 0:
+                for s in range(PACK, NSLICE):
+                    fetch_whips(s)
+            for b in range(NBLK):
+                second_stage(jt, b)
+            if jt % 2 == 1:
+                third_stage(jt // 2)

@@ -20,10 +20,21 @@ ALU = mybir.AluOpType
 
 P = 128
 PACK = 4
-BLOCK = P * PACK
-NBLK = H // BLOCK
+ROWS = P * PACK
+NGRP = H // ROWS
 NSLICE = H // P
+QUADS, QUAD = 4, 32
+LIST_ROWS = 16
+RUN = 4
+JT = NP // P
 ROUNDER = 1.5 * 2.0**23
+
+RAW_BUFS = 3
+WOVEN_W_BUFS = 3
+H_BUFS = 6
+GATE_BUFS = 5
+T_BUFS = 3
+XS_LOW_AFTER = 5
 
 
 def tile_list_division_member_page_kernel(
@@ -35,43 +46,52 @@ def tile_list_division_member_page_kernel(
         keep = ctx.enter_context(tc.tile_pool(name="keep", bufs=1))
         ring = ctx.enter_context(tc.tile_pool(name="ring", bufs=2))
         psum = ctx.enter_context(tc.psum_pool(name="psum", bufs=2))
+        bank_tags = ["bank_a", "bank_b", "bank_c", "bank_d"]
 
         def kept(shape, dtype, name, tag=None):
             return keep.tile(shape, dtype, name=name, tag=tag or name, align_bytes=64)
 
         def load_list(src, name):
-            tile = keep.tile([P, S // 16], U16, name=name)
+            tile = keep.tile([P, S // LIST_ROWS], U16, name=name)
             nc.sync.dma_start(tile[:], src)
             return tile
 
-        def load_scale_rows(queues, plane, src):
-            for quad in range(4):
-                queues[quad].dma_start(
-                    plane[32 * quad : 32 * quad + 4, :].bitcast(I32), src[0, 4 * quad : 4 * quad + 4, :].bitcast(I32)
-                )
+        def load_scale_rows(plane, src):
+            passes = src.shape[0]
+            for quad in range(QUADS):
+                blocks = slice(PACK * quad, PACK * (quad + 1))
+                rows = src[:, blocks, :] if passes > 1 else src[0, blocks, :]
+                nc.sync.dma_start(plane[QUAD * quad : QUAD * quad + PACK * passes, :].bitcast(I32), rows.bitcast(I32))
 
-        def load_weight_block(w, a, b, name):
-            raw = ring.tile([P, PACK, BLOCK], F32, name=name, tag="raw", bufs=4)
-            rows = w[BLOCK * a : BLOCK * (a + 1), BLOCK * b : BLOCK * (b + 1)]
-            nc.sync.dma_start(raw[:], rows.rearrange("(p i) c -> p i c", i=PACK))
+        def load_weight_piece(w, a, b, name):
+            raw = ring.tile([P, PACK, ROWS], F32, name=name, tag="raw", bufs=RAW_BUFS)
+            piece = w[ROWS * a : ROWS * (a + 1), ROWS * b : ROWS * (b + 1)]
+            nc.sync.dma_start(raw[:], piece.rearrange("(p i) c -> p i c", i=PACK))
             return raw
 
         def load_wb_words(b):
-            raw = kept([P, 2 * BLOCK], U8, "wb_raw%d" % b)
-            nc.sync.dma_start(raw[:].bitcast(I32), wb_words[0, :, 2 * BLOCK * b : 2 * BLOCK * (b + 1)].bitcast(I32))
+            raw = kept([P, 2 * ROWS], U8, "wb_raw%d" % b)
+            nc.sync.dma_start(raw[:].bitcast(I32), wb_words[0, :, 2 * ROWS * b : 2 * ROWS * (b + 1)].bitcast(I32))
             return raw
 
         def load_page(s):
             a, i = divmod(s, PACK)
             page = kept([P, T2], F32, "page%d" % s)
-            rows = page0[BLOCK * a : BLOCK * (a + 1), :].rearrange("(p i) c -> p i c", i=PACK)
-            nc.sync.dma_start(page[:], rows[:, i, :])
+            group = page0[ROWS * a : ROWS * (a + 1), :].rearrange("(p i) c -> p i c", i=PACK)
+            nc.sync.dma_start(page[:], group[:, i, :])
             return page
 
         def load_vector(vec, name):
-            tile = kept([P, NBLK, PACK], F32, name)
-            nc.gpsimd.dma_start(tile[:], vec.rearrange("(a p i) -> p a i", p=P, i=PACK))
+            tile = kept([P, NGRP, PACK], F32, name)
+            nc.sync.dma_start(tile[:], vec.rearrange("(a p i) -> p a i", p=P, i=PACK))
             return tile
+
+        def load_wgs(places):
+            for quad in range(QUADS):
+                nc.sync.dma_start(
+                    wgs_t[QUAD * quad : QUAD * (quad + 1), places, :],
+                    wgs.rearrange("(p i) j -> p i j", i=PACK)[:, places, :],
+                )
 
         tab_plane = kept([P, T], U8, "tab_plane")
         wb_plane_raw = kept([P, H], U8, "wb_plane_raw")
@@ -82,39 +102,39 @@ def tile_list_division_member_page_kernel(
 
         idx = load_list(offs, "idx")
         wb_raw = [load_wb_words(0)]
-        load_scale_rows([nc.sync] * 4, wb_plane_raw, wb_scales)
+        load_scale_rows(wb_plane_raw, wb_scales)
         tab_codes = kept([P, T], I32, "tab_codes")
         nc.sync.dma_start(tab_codes[:], tab_words[0].rearrange("p t i -> p (t i)").bitcast(I32))
-        load_scale_rows([nc.sync] * 4, tab_plane, tab_scales)
+        load_scale_rows(tab_plane, tab_scales)
         ident = kept([P, P], F32, "ident")
         make_identity(nc, ident[:])
-        gain_t = load_vector(gain, "gain_t")
-        sc_t = load_vector(sc, "sc_t")
-        wv_t = load_vector(wv, "wv_t")
+        warm = kept([P, 1], F32, "warm")
+        nc.scalar.activation(warm[:], ident[:, 0:1], ACT.Silu)
 
-        wa_raw = [load_weight_block(wa, 0, 0, "wa_raw0")]
+        wa_raw = [load_weight_piece(wa, 0, 0, "wa_raw0")]
+        gain_t = load_vector(gain, "gain_t")
+        wa_raw.append(load_weight_piece(wa, 0, 1, "wa_raw1"))
         wb_raw.append(load_wb_words(1))
         pages = [load_page(0)]
         wgs_t = kept([P, PACK, S], F32, "wgs_t")
-        for quad in range(4):
-            nc.sync.dma_start(wgs_t[32 * quad : 32 * (quad + 1), :, :], wgs.rearrange("(p i) j -> p i j", i=PACK))
         idx2 = load_list(offs2, "idx2")
+        load_wgs(slice(0, 1))
         idx3 = load_list(offs3, "idx3")
         idx4 = load_list(offs4, "idx4")
-        wa_raw.append(load_weight_block(wa, 0, 1, "wa_raw1"))
+        pages.append(load_page(1))
+        load_wgs(slice(1, PACK))
+        w2_pieces = [(a, b) for a in range(NGRP) for b in range(NGRP)]
         w2_raw = {}
-        for s in range(1, NSLICE):
+        for s in range(2, NSLICE):
             pages.append(load_page(s))
-            if s % 2 == 1:
-                a, b = divmod(s // 2, NBLK)
-                w2_raw[(a, b)] = load_weight_block(w2, a, b, "w2_raw%d%d" % (a, b))
-        w3_raw = kept([P, NBLK, H], I32, "w3_raw")
+            if len(w2_raw) < len(w2_pieces):
+                a, b = w2_pieces[len(w2_raw)]
+                w2_raw[(a, b)] = load_weight_piece(w2, a, b, "w2_raw%d%d" % (a, b))
+        sc_t = load_vector(sc, "sc_t")
+        wv_t = load_vector(wv, "wv_t")
+        w3_raw = kept([P, NGRP, H], I32, "w3_raw")
         nc.sync.dma_start(w3_raw[:], w3_words.rearrange("a p n i -> p a (n i)").bitcast(I32))
-        for quad in range(4):
-            nc.sync.dma_start(
-                w3_plane_raw[32 * quad : 32 * quad + 4 * NBLK, :].bitcast(I32),
-                w3_scales[:, 4 * quad : 4 * quad + 4, :].bitcast(I32),
-            )
+        load_scale_rows(w3_plane_raw, w3_scales)
 
         v_codes = kept([P, S], U32, "v_codes")
         v_plane = kept([P, S], U8, "v_plane")
@@ -123,16 +143,16 @@ def tile_list_division_member_page_kernel(
 
         def deal_wb(b):
             nc.vector.tensor_copy(
-                wb_codes[:].rearrange("p (b i q e) -> p b i q e", b=NBLK, i=PACK, e=2)[:, b],
+                wb_codes[:].rearrange("p (b i q e) -> p b i q e", b=NGRP, i=PACK, e=2)[:, b],
                 wb_raw[b][:].rearrange("p (q i e) -> p i q e", i=PACK, e=2),
             )
             nc.vector.tensor_copy(
-                wb_plane[:].rearrange("p (b i q) -> p b i q", b=NBLK, i=PACK)[:, b],
-                wb_plane_raw[:].rearrange("p (b q i) -> p b i q", b=NBLK, i=PACK)[:, b],
+                wb_plane[:].rearrange("p (b i q) -> p b i q", b=NGRP, i=PACK)[:, b],
+                wb_plane_raw[:].rearrange("p (b q i) -> p b i q", b=NGRP, i=PACK)[:, b],
             )
 
-        def entries(tile, js):
-            return tile[:, js.start // 16 : js.stop // 16]
+        def entries(list_tile, js):
+            return list_tile[:, js.start // LIST_ROWS : js.stop // LIST_ROWS]
 
         halves = [slice(0, S // 2), slice(S // 2, S)]
         deal_wb(0)
@@ -140,25 +160,26 @@ def tile_list_division_member_page_kernel(
             nc.vector.tensor_copy(v_codes[:, js], tab_codes[:].bitcast(U32).indirect(entries(idx, js)))
             nc.vector.tensor_copy(v_plane[:, js], tab_plane[:].indirect(entries(idx, js)))
 
-        def cast_views(raw, grouped, qs):
-            dst = grouped[:].rearrange("p (t q i) -> p q i t", t=PACK, i=PACK)[:, qs]
-            src = raw[:].rearrange("p i (q t) -> p q i t", t=PACK)[:, qs]
+        def deal_and_weave_views(raw, woven_w, qs):
+            dst = woven_w[:].rearrange("p (u q i) -> p q i u", u=PACK, i=PACK)[:, qs]
+            src = raw[:].rearrange("p i (q u) -> p q i u", u=PACK)[:, qs]
             return dst, src
 
-        def quantise(codes, plane, grouped):
-            nc.vector.quantize_mx(out=codes.bitcast(FP8X4), scales=plane, in_=grouped)
+        def quantise(codes, plane, values):
+            nc.vector.quantize_mx(out=codes.bitcast(FP8X4), scales=plane, in_=values)
+
+        def woven_weight_tile(name):
+            return ring.tile([P, PACK * ROWS], BF16, name=name, tag="woven_w", bufs=WOVEN_W_BUFS, align_bytes=64)
 
         wa_codes = kept([P, H], U32, "wa_codes")
         wa_plane = kept([P, H], U8, "wa_plane")
-
-        def prepare_wa(b):
-            grouped = ring.tile([P, PACK * BLOCK], BF16, name="wa_grouped", tag="grouped", align_bytes=64)
-            dst, src = cast_views(wa_raw[b], grouped, slice(0, P))
+        for b in range(NGRP):
+            wa_woven = woven_weight_tile("wa_woven")
+            dst, src = deal_and_weave_views(wa_raw[b], wa_woven, slice(0, P))
             nc.vector.tensor_copy(dst, src)
-            cols = slice(BLOCK * b, BLOCK * (b + 1))
-            quantise(wa_codes[:, cols], wa_plane[:, cols], grouped[:])
-
-        prepare_wa(0)
+            cols = slice(ROWS * b, ROWS * (b + 1))
+            quantise(wa_codes[:, cols], wa_plane[:, cols], wa_woven[:])
+        deal_wb(1)
 
         def add_transposed(bank, first, second, n):
             for jt in range(n // P):
@@ -166,21 +187,23 @@ def tile_list_division_member_page_kernel(
                 nc.tensor.matmul(bank[:, cols], first[:, cols], ident[:], start=True, stop=False, is_transpose=True)
                 nc.tensor.matmul(bank[:, cols], second[:, cols], ident[:], start=False, stop=True, is_transpose=True)
 
-        x = [kept([P, PACK, NP], F32, "x%d" % a) for a in range(NBLK)]
-        whips = [kept([P, PACK, NP], F32, "whips0")]
-        w2_codes = [kept([P, H], U32, "w2_codes%d" % a) for a in range(NBLK)]
-        w2_plane = [kept([P, H], U8, "w2_plane%d" % a) for a in range(NBLK)]
-        xs_codes = [kept([P, NP], U32, "xs_codes%d" % a) for a in range(NBLK)]
-        xs_plane = [kept([P, NP], U8, "xs_plane%d" % a) for a in range(NBLK)]
-        t_codes = [kept([P, NP], U32, "t_codes%d" % a) for a in range(NBLK)]
-        t_plane = [kept([P, NP], U8, "t_plane%d" % a) for a in range(NBLK)]
-        w2_grouped = {}
+        x = [kept([P, PACK, NP], F32, "x%d" % a) for a in range(NGRP)]
+        whips = [kept([P, 2, NP], F32, "whips%d" % pair) for pair in range(2)]
+        w2_codes = [kept([P, H], U32, "w2_codes%d" % a) for a in range(NGRP)]
+        w2_plane = [kept([P, H], U8, "w2_plane%d" % a) for a in range(NGRP)]
+        xs_codes = {1: kept([P, NP], U32, "xs_codes1")}
+        xs_plane = [kept([P, NP], U8, "xs_plane%d" % a) for a in range(NGRP)]
+        t_codes = [kept([P, NP], U32, "t_codes%d" % a) for a in range(NGRP)]
+        t_plane = [kept([P, NP], U8, "t_plane%d" % a) for a in range(NGRP)]
+        xs = []
+        last = NSLICE - 1
+        lin_tags = {XS_LOW_AFTER: "xs0", last: "xs1"}
 
         def new_entries(s, js):
             a, i = divmod(s, PACK)
             n = js.stop - js.start
             rows = slice(P * s, P * (s + 1))
-            ang = psum.tile([P, n], F32, name="ang", tag="bank_a")
+            ang = psum.tile([P, n], F32, name="ang", tag=bank_tags[0])
             nc.tensor.matmul_mx(
                 out=ang[:], lhsT=wb_codes[:, 2 * P * s : 2 * P * (s + 1)].bitcast(FP4X4), lhsT_scale=wb_plane[:, rows],
                 rhs=v_codes[:, js].bitcast(FP8X4), rhs_scale=v_plane[:, js], start=True, stop=True,
@@ -191,24 +214,27 @@ def tile_list_division_member_page_kernel(
             nc.scalar.activation(whole[:], turns[:], ACT.Copy, bias=ROUNDER, scale=1.0)
             minus = ring.tile([P, n], F32, name="minus")
             nc.scalar.activation(minus[:], whole[:], ACT.Copy, bias=ROUNDER, scale=-1.0)
-            frac = psum.tile([P, n], F32, name="frac", tag="bank_b")
+            frac = psum.tile([P, n], F32, name="frac", tag=bank_tags[1])
             add_transposed(frac, turns, minus, n)
-            lin = psum.tile([P, n], F32, name="lin", tag="bank_c")
+            lin = psum.tile([P, n], F32, name="lin", tag=bank_tags[0] if js.start > 0 else bank_tags[2])
             for jt in range(n // P):
                 cols = slice(js.start + P * jt, js.start + P * (jt + 1))
                 nc.tensor.matmul_mx(
                     out=lin[:, P * jt : P * (jt + 1)], lhsT=v_codes[:, cols].bitcast(FP8X4), lhsT_scale=v_plane[:, cols],
                     rhs=wa_codes[:, rows].bitcast(FP8X4), rhs_scale=wa_plane[:, rows], start=True, stop=True,
                 )
-            cos_t = ring.tile([P, n], F32, name="cos_t")
+            cos_t = kept([P, n], F32, "cos_t", "xs_codes0") if s == last else ring.tile([P, n], F32, name="cos_t")
             nc.scalar.activation(cos_t[:], frac[:], ACT.Sin, scale=2.0 * math.pi)
-            lin_t = ring.tile([P, n], F32, name="lin_t")
+            lin_t = kept([P, n], F32, "lin_t", lin_tags[s]) if s in lin_tags else ring.tile([P, n], F32, name="lin_t")
             nc.scalar.copy(lin_t[:], lin[:])
-            total = psum.tile([P, n], F32, name="total", tag="bank_d")
+            total = psum.tile([P, n], F32, name="total", tag=bank_tags[3])
             add_transposed(total, cos_t, lin_t, n)
-            h = ring.tile([P, n], F32, name="h", bufs=NSLICE)
+            h = ring.tile([P, n], F32, name="h", bufs=H_BUFS)
             nc.scalar.activation(h[:], total[:], ACT.Copy, scale=gain_t[:, a, i : i + 1])
-            nc.vector.tensor_tensor(pages[s][:].indirect(entries(idx2, js)), h[:], wgs_t[:, i, js], ALU.mult)
+            return h
+
+        def put_entries(s, js, h):
+            nc.vector.tensor_tensor(pages[s][:].indirect(entries(idx2, js)), h[:], wgs_t[:, s % PACK, js], ALU.mult)
 
         def fetch_x(s):
             a, i = divmod(s, PACK)
@@ -219,112 +245,121 @@ def tile_list_division_member_page_kernel(
             nc.scalar.activation(xs[a][:, i, :], x[a][:, i, :], ACT.Copy, scale=sc_t[:, a, i : i + 1])
 
         def fetch_whips(s):
-            a, i = divmod(s, PACK)
-            nc.vector.tensor_copy(whips[a][:, i, :], pages[s][:].indirect(idx4[:]))
+            nc.vector.tensor_copy(whips[s // 2][:, s % 2, :], pages[s][:].indirect(idx4[:]))
 
-        def cast_w2(piece):
-            blk, half = divmod(piece, 2)
-            a, b = divmod(blk, NBLK)
-            if half == 0:
-                w2_grouped[blk] = ring.tile([P, PACK * BLOCK], BF16, name="w2_grouped", tag="grouped", align_bytes=64)
-            dst, src = cast_views(w2_raw[(a, b)], w2_grouped[blk], slice(64 * half, 64 * (half + 1)))
-            nc.scalar.copy(dst, src)
-            if half == 1:
-                cols = slice(BLOCK * b, BLOCK * (b + 1))
-                quantise(w2_codes[a][:, cols], w2_plane[a][:, cols], w2_grouped[blk][:])
+        def prepare_w2(a, b):
+            w2_woven = woven_weight_tile("w2_woven")
+            for qs in (slice(0, P // 2), slice(P // 2, P)):
+                dst, src = deal_and_weave_views(w2_raw[(a, b)], w2_woven, qs)
+                nc.scalar.copy(dst, src)
+            cols = slice(ROWS * b, ROWS * (b + 1))
+            quantise(w2_codes[a][:, cols], w2_plane[a][:, cols], w2_woven[:])
 
-        def walk(four_rows):
-            return four_rows.rearrange("p i (c e) -> p c i e", e=4)
+        def walk(four_slices):
+            return four_slices.rearrange("p i (c e) -> p c i e", e=RUN)
 
         def woven(flat):
-            return flat.rearrange("p (c e i) -> p c i e", e=4, i=PACK)
+            return flat.rearrange("p (c e i) -> p c i e", e=RUN, i=PACK)
 
-        def quantise_xs(a, jt):
+        def weave_xs(a, jt):
+            xs_woven = ring.tile([P, PACK * P], BF16, name="xs_woven", bufs=NGRP * JT, align_bytes=64)
+            nc.scalar.copy(woven(xs_woven[:]), walk(xs[a][:, :, P * jt : P * (jt + 1)]))
+            return xs_woven
+
+        def quantise_xs(a, jt, xs_woven):
             cols = slice(P * jt, P * (jt + 1))
-            xs_woven = ring.tile([P, PACK * P], BF16, name="xs_woven", bufs=3, align_bytes=64)
-            nc.scalar.copy(woven(xs_woven[:]), walk(xs[a][:, :, cols]))
             quantise(xs_codes[a][:, cols], xs_plane[a][:, cols], xs_woven[:])
 
+        w2_after = {2: w2_pieces[0:1], 3: w2_pieces[1:2], last: w2_pieces[2:]}
         for s in range(NSLICE):
+            if s == last:
+                xs.append(kept([P, PACK, NP], BF16, "xs0"))
+                for low in range(PACK):
+                    scale_x(low)
+                xs_low_woven = [weave_xs(0, jt) for jt in range(JT)]
             for js in halves if s == 0 else [slice(0, S)]:
-                new_entries(s, js)
+                h = new_entries(s, js)
+                if s == last:
+                    xs_codes[0] = kept([P, NP], U32, "xs_codes0")
+                    for jt in range(JT):
+                        quantise_xs(0, jt, xs_low_woven[jt])
+                put_entries(s, js, h)
             fetch_x(s)
-            if s == 0:
-                deal_wb(1)
-                prepare_wa(1)
             if s < PACK:
                 fetch_whips(s)
-            if s > 0:
-                cast_w2(s - 1)
-        cast_w2(NSLICE - 1)
-        xs = [kept([P, PACK, NP], BF16, "xs0", "wa_codes"), kept([P, PACK, NP], BF16, "xs1", "wb_codes")]
-        whips.append(kept([P, PACK, NP], F32, "whips1", "wgs_t"))
-        for s in range(PACK):
-            scale_x(s)
-        for jt in range(PACK):
-            quantise_xs(0, jt)
+            for a, b in w2_after.get(s, []):
+                prepare_w2(a, b)
+        xs.append(kept([P, PACK, NP], BF16, "xs1"))
+        whips.append(kept([P, 2, NP], F32, "whips2", "wgs_t"))
         for s in range(PACK, NSLICE):
             scale_x(s)
 
-        w3_codes = kept([P, NBLK, H], I32, "w3_codes")
-        w3_plane = kept([P, H], U8, "w3_plane")
-        nc.vector.tensor_copy(
-            w3_codes[:].rearrange("p a (b i q) -> p (a b) q i", b=NBLK, i=PACK),
-            w3_raw[:].rearrange("p a (b q i) -> p (a b) q i", b=NBLK, i=PACK),
-        )
-        nc.vector.tensor_copy(
-            w3_plane[:].rearrange("p (b i q) -> p b i q", b=NBLK, i=PACK),
-            w3_plane_raw[:].rearrange("p (b q i) -> p b i q", b=NBLK, i=PACK),
-        )
+        pre_tanh = {}
 
-        def second_stage(jt, b):
+        def second_stage_pass(jt, b, a):
             cols = slice(P * jt, P * (jt + 1))
-            bank = psum.tile([P, PACK, P], F32, name="pre_tanh", tag="bank_a" if b == 0 else "bank_b")
             for i in range(PACK):
-                rows = slice(BLOCK * b + P * i, BLOCK * b + P * (i + 1))
-                for a in range(NBLK):
-                    nc.tensor.matmul_mx(
-                        out=bank[:, i, :], lhsT=w2_codes[a][:, rows].bitcast(FP8X4), lhsT_scale=w2_plane[a][:, rows],
-                        rhs=xs_codes[a][:, cols].bitcast(FP8X4), rhs_scale=xs_plane[a][:, cols],
-                        start=(a == 0), stop=(a == NBLK - 1),
-                    )
-            gate = ring.tile([P, PACK * P], F32, name="gate", bufs=3)
-            gate_walk = gate[:].rearrange("p (c i e) -> p c i e", i=PACK, e=4)
-            nc.scalar.activation(gate_walk, walk(bank[:]), ACT.Tanh)
-            t_woven = ring.tile([P, PACK * P], BF16, name="t_woven", bufs=3, align_bytes=64)
+                rows = slice(ROWS * b + P * i, ROWS * b + P * (i + 1))
+                nc.tensor.matmul_mx(
+                    out=pre_tanh[(jt, b)][:, i, :], lhsT=w2_codes[a][:, rows].bitcast(FP8X4),
+                    lhsT_scale=w2_plane[a][:, rows],
+                    rhs=xs_codes[a][:, cols].bitcast(FP8X4), rhs_scale=xs_plane[a][:, cols],
+                    start=(a == 0 and i == 0), stop=(a == NGRP - 1 and i == PACK - 1),
+                )
+
+        def gate_and_quantise(jt, b):
+            cols = slice(P * jt, P * (jt + 1))
+            gate = ring.tile([P, PACK * P], F32, name="gate", bufs=GATE_BUFS)
+            gate_walk = gate[:].rearrange("p (c i e) -> p c i e", i=PACK, e=RUN)
+            nc.scalar.activation(gate_walk, walk(pre_tanh[(jt, b)][:]), ACT.Tanh)
+            t_woven = ring.tile([P, PACK * P], BF16, name="t_woven", bufs=T_BUFS, align_bytes=64)
             nc.vector.tensor_tensor(woven(t_woven[:]), gate_walk, walk(x[b][:, :, cols]), ALU.mult)
             quantise(t_codes[b][:, cols], t_plane[b][:, cols], t_woven[:])
 
-        def third_stage(half):
-            cols = slice(2 * P * half, 2 * P * (half + 1))
-            for b in range(NBLK):
-                for pair in range(2):
-                    bank = psum.tile([P, 2, 2 * P], F32, name="y", tag="bank_c" if pair == 0 else "bank_d")
-                    res = ring.tile([P, 2, 2 * P], F32, name="res", bufs=4)
-                    for k in range(2):
-                        i = 2 * pair + k
-                        rows = slice(BLOCK * b + P * i, BLOCK * b + P * (i + 1))
-                        for a in range(NBLK):
-                            nc.tensor.matmul_mx(
-                                out=bank[:, k, :], lhsT=w3_codes[:, a, rows].bitcast(FP8X4),
-                                lhsT_scale=w3_plane[4 * a : P, rows],
-                                rhs=t_codes[a][:, cols].bitcast(FP8X4), rhs_scale=t_plane[a][:, cols],
-                                start=(a == 0), stop=(a == NBLK - 1),
-                            )
-                    for k in range(2):
-                        i = 2 * pair + k
-                        nc.vector.scalar_tensor_tensor(
-                            res[:, k, :], whips[b][:, i, cols], wv_t[:, b, i : i + 1], bank[:, k, :], ALU.mult, ALU.add
-                        )
-                    dst = out[BLOCK * b : BLOCK * (b + 1), cols].rearrange("(p i) j -> p i j", i=PACK)
-                    nc.sync.dma_start(dst[:, 2 * pair : 2 * pair + 2, :], res[:])
+        for jt in range(JT):
+            for b in range(NGRP):
+                tag = bank_tags[(NGRP * jt + b) % len(bank_tags)]
+                pre_tanh[(jt, b)] = psum.tile([P, PACK, P], F32, name="pre_tanh", tag=tag)
+                second_stage_pass(jt, b, 0)
+        for jt in range(JT):
+            quantise_xs(1, jt, weave_xs(1, jt))
+        for jt in range(JT):
+            for b in range(NGRP):
+                second_stage_pass(jt, b, 1)
+                gate_and_quantise(jt, b)
+        whips.append(kept([P, 2, NP], F32, "whips3", "xs1"))
+        for s in range(PACK, NSLICE):
+            fetch_whips(s)
 
-        for jt in range(PACK):
-            quantise_xs(1, jt)
-            if jt == 0:
-                for s in range(PACK, NSLICE):
-                    fetch_whips(s)
-            for b in range(NBLK):
-                second_stage(jt, b)
-            if jt % 2 == 1:
-                third_stage(jt // 2)
+        w3_codes = kept([P, NGRP, H], I32, "w3_codes", "xs0")
+        w3_plane = kept([P, H], U8, "w3_plane", "wa_plane")
+        nc.vector.tensor_copy(
+            w3_codes[:].rearrange("p a (b i q) -> p (a b) q i", b=NGRP, i=PACK),
+            w3_raw[:].rearrange("p a (b q i) -> p (a b) q i", b=NGRP, i=PACK),
+        )
+        nc.vector.tensor_copy(
+            w3_plane[:].rearrange("p (b i q) -> p b i q", b=NGRP, i=PACK),
+            w3_plane_raw[:].rearrange("p (b q i) -> p b i q", b=NGRP, i=PACK),
+        )
+        for cols in halves:
+            for pair in range(NSLICE // 2):
+                slices = (2 * pair, 2 * pair + 1)
+                b, i0 = divmod(slices[0], PACK)
+                y = psum.tile([P, 2, NP // 2], F32, name="y", tag=bank_tags[pair])
+                res = ring.tile([P, 2, NP // 2], F32, name="res", bufs=NSLICE)
+                for a in range(NGRP):
+                    for k, s in enumerate(slices):
+                        rows = slice(P * s, P * (s + 1))
+                        nc.tensor.matmul_mx(
+                            out=y[:, k, :], lhsT=w3_codes[:, a, rows].bitcast(FP8X4),
+                            lhsT_scale=w3_plane[PACK * a : P, rows],
+                            rhs=t_codes[a][:, cols].bitcast(FP8X4), rhs_scale=t_plane[a][:, cols],
+                            start=(a == 0 and k == 0), stop=(a == NGRP - 1 and k == 1),
+                        )
+                for k in range(2):
+                    nc.vector.scalar_tensor_tensor(
+                        res[:, k, :], whips[pair][:, k, cols], wv_t[:, b, i0 + k : i0 + k + 1], y[:, k, :],
+                        ALU.mult, ALU.add,
+                    )
+                group = out[ROWS * b : ROWS * (b + 1), cols].rearrange("(p i) j -> p i j", i=PACK)
+                nc.sync.dma_start(group[:, i0 : i0 + 2, :], res[:])

import math
from contextlib import ExitStack

import concourse.mybir as mybir
from concourse.masks import make_identity

K, T, S, H, T2, NP = 512, 2048, 512, 1024, 1024, 512
FLOPS = 2 * (2 * K * H * S + 2 * H * H * NP)

F32 = mybir.dt.float32
BF16 = mybir.dt.bfloat16
I32 = mybir.dt.int32
U32 = mybir.dt.uint32
U16 = mybir.dt.uint16
U8 = mybir.dt.uint8
FP8X4 = mybir.dt.float8_e4m3fn_x4
FP4X4 = mybir.dt.float4_e2m1fn_x4
ACT = mybir.ActivationFunctionType
ALU = mybir.AluOpType

P = 128
PACK = 4
ROWS = P * PACK
NGRP = H // ROWS
NSLICE = H // P
QUADS, QUAD = 4, 32
LIST_ROWS = 16
RUN = 4
JT = NP // P
ROUNDER = 1.5 * 2.0**23

RAW_BUFS = 3
WOVEN_W_BUFS = 3
H_BUFS = 6
GATE_BUFS = 5
T_BUFS = 3
XS_LOW_AFTER = 5


def tile_list_division_member_page_kernel(
    tc, tab_words, tab_scales, offs, wa, wb_words, wb_scales, gain, page0, wgs, offs2, offs3, offs4, sc, w2,
    w3_words, w3_scales, wv, out,
):
    nc = tc.nc
    with ExitStack() as ctx:
        keep = ctx.enter_context(tc.tile_pool(name="keep", bufs=1))
        ring = ctx.enter_context(tc.tile_pool(name="ring", bufs=2))
        psum = ctx.enter_context(tc.psum_pool(name="psum", bufs=2))
        bank_tags = ["bank_a", "bank_b", "bank_c", "bank_d"]

        def kept(shape, dtype, name, tag=None):
            return keep.tile(shape, dtype, name=name, tag=tag or name, align_bytes=64)

        def load_list(src, name):
            tile = keep.tile([P, S // LIST_ROWS], U16, name=name)
            nc.sync.dma_start(tile[:], src)
            return tile

        def load_scale_rows(plane, src):
            passes = src.shape[0]
            for quad in range(QUADS):
                blocks = slice(PACK * quad, PACK * (quad + 1))
                rows = src[:, blocks, :] if passes > 1 else src[0, blocks, :]
                nc.sync.dma_start(plane[QUAD * quad : QUAD * quad + PACK * passes, :].bitcast(I32), rows.bitcast(I32))

        def load_weight_piece(w, a, b, name):
            raw = ring.tile([P, PACK, ROWS], F32, name=name, tag="raw", bufs=RAW_BUFS)
            piece = w[ROWS * a : ROWS * (a + 1), ROWS * b : ROWS * (b + 1)]
            nc.sync.dma_start(raw[:], piece.rearrange("(p i) c -> p i c", i=PACK))
            return raw

        def load_wb_words(b):
            raw = kept([P, 2 * ROWS], U8, "wb_raw%d" % b)
            nc.sync.dma_start(raw[:].bitcast(I32), wb_words[0, :, 2 * ROWS * b : 2 * ROWS * (b + 1)].bitcast(I32))
            return raw

        def load_page(s):
            a, i = divmod(s, PACK)
            page = kept([P, T2], F32, "page%d" % s)
            group = page0[ROWS * a : ROWS * (a + 1), :].rearrange("(p i) c -> p i c", i=PACK)
            nc.sync.dma_start(page[:], group[:, i, :])
            return page

        def load_vector(vec, name):
            tile = kept([P, NGRP, PACK], F32, name)
            nc.sync.dma_start(tile[:], vec.rearrange("(a p i) -> p a i", p=P, i=PACK))
            return tile

        def load_wgs(places):
            for quad in range(QUADS):
                nc.sync.dma_start(
                    wgs_t[QUAD * quad : QUAD * (quad + 1), places, :],
                    wgs.rearrange("(p i) j -> p i j", i=PACK)[:, places, :],
                )

        tab_plane = kept([P, T], U8, "tab_plane")
        wb_plane_raw = kept([P, H], U8, "wb_plane_raw")
        w3_plane_raw = kept([P, H], U8, "w3_plane_raw")
        nc.gpsimd.memset(wb_plane_raw[:].bitcast(I32), 0)
        nc.gpsimd.memset(tab_plane[:].bitcast(I32), 0)
        nc.vector.memset(w3_plane_raw[:].bitcast(I32), 0)

        idx = load_list(offs, "idx")
        wb_raw = [load_wb_words(0)]
        load_scale_rows(wb_plane_raw, wb_scales)
        tab_codes = kept([P, T], I32, "tab_codes")
        nc.sync.dma_start(tab_codes[:], tab_words[0].rearrange("p t i -> p (t i)").bitcast(I32))
        load_scale_rows(tab_plane, tab_scales)
        ident = kept([P, P], F32, "ident")
        make_identity(nc, ident[:])
        warm = kept([P, 1], F32, "warm")
        nc.scalar.activation(warm[:], ident[:, 0:1], ACT.Silu)

        wa_raw = [load_weight_piece(wa, 0, 0, "wa_raw0")]
        gain_t = load_vector(gain, "gain_t")
        wa_raw.append(load_weight_piece(wa, 0, 1, "wa_raw1"))
        wb_raw.append(load_wb_words(1))
        pages = [load_page(0)]
        wgs_t = kept([P, PACK, S], F32, "wgs_t")
        idx2 = load_list(offs2, "idx2")
        load_wgs(slice(0, 1))
        idx3 = load_list(offs3, "idx3")
        idx4 = load_list(offs4, "idx4")
        pages.append(load_page(1))
        load_wgs(slice(1, PACK))
        w2_pieces = [(a, b) for a in range(NGRP) for b in range(NGRP)]
        w2_raw = {}
        for s in range(2, NSLICE):
            pages.append(load_page(s))
            if len(w2_raw) < len(w2_pieces):
                a, b = w2_pieces[len(w2_raw)]
                w2_raw[(a, b)] = load_weight_piece(w2, a, b, "w2_raw%d%d" % (a, b))
        sc_t = load_vector(sc, "sc_t")
        wv_t = load_vector(wv, "wv_t")
        w3_raw = kept([P, NGRP, H], I32, "w3_raw")
        nc.sync.dma_start(w3_raw[:], w3_words.rearrange("a p n i -> p a (n i)").bitcast(I32))
        load_scale_rows(w3_plane_raw, w3_scales)

        v_codes = kept([P, S], U32, "v_codes")
        v_plane = kept([P, S], U8, "v_plane")
        wb_codes = kept([P, 2 * H], U8, "wb_codes")
        wb_plane = kept([P, H], U8, "wb_plane")

        def deal_wb(b):
            nc.vector.tensor_copy(
                wb_codes[:].rearrange("p (b i q e) -> p b i q e", b=NGRP, i=PACK, e=2)[:, b],
                wb_raw[b][:].rearrange("p (q i e) -> p i q e", i=PACK, e=2),
            )
            nc.vector.tensor_copy(
                wb_plane[:].rearrange("p (b i q) -> p b i q", b=NGRP, i=PACK)[:, b],
                wb_plane_raw[:].rearrange("p (b q i) -> p b i q", b=NGRP, i=PACK)[:, b],
            )

        def entries(list_tile, js):
            return list_tile[:, js.start // LIST_ROWS : js.stop // LIST_ROWS]

        halves = [slice(0, S // 2), slice(S // 2, S)]
        deal_wb(0)
        for js in halves:
            nc.vector.tensor_copy(v_codes[:, js], tab_codes[:].bitcast(U32).indirect(entries(idx, js)))
            nc.vector.tensor_copy(v_plane[:, js], tab_plane[:].indirect(entries(idx, js)))

        def deal_and_weave_views(raw, woven_w, qs):
            dst = woven_w[:].rearrange("p (u q i) -> p q i u", u=PACK, i=PACK)[:, qs]
            src = raw[:].rearrange("p i (q u) -> p q i u", u=PACK)[:, qs]
            return dst, src

        def quantise(codes, plane, values):
            nc.vector.quantize_mx(out=codes.bitcast(FP8X4), scales=plane, in_=values)

        def woven_weight_tile(name):
            return ring.tile([P, PACK * ROWS], BF16, name=name, tag="woven_w", bufs=WOVEN_W_BUFS, align_bytes=64)

        wa_codes = kept([P, H], U32, "wa_codes")
        wa_plane = kept([P, H], U8, "wa_plane")
        for b in range(NGRP):
            wa_woven = woven_weight_tile("wa_woven")
            dst, src = deal_and_weave_views(wa_raw[b], wa_woven, slice(0, P))
            nc.vector.tensor_copy(dst, src)
            cols = slice(ROWS * b, ROWS * (b + 1))
            quantise(wa_codes[:, cols], wa_plane[:, cols], wa_woven[:])
        deal_wb(1)

        def add_transposed(bank, first, second, n):
            for jt in range(n // P):
                cols = slice(P * jt, P * (jt + 1))
                nc.tensor.matmul(bank[:, cols], first[:, cols], ident[:], start=True, stop=False, is_transpose=True)
                nc.tensor.matmul(bank[:, cols], second[:, cols], ident[:], start=False, stop=True, is_transpose=True)

        x = [kept([P, PACK, NP], F32, "x%d" % a) for a in range(NGRP)]
        whips = [kept([P, 2, NP], F32, "whips%d" % pair) for pair in range(2)]
        w2_codes = [kept([P, H], U32, "w2_codes%d" % a) for a in range(NGRP)]
        w2_plane = [kept([P, H], U8, "w2_plane%d" % a) for a in range(NGRP)]
        xs_codes = {1: kept([P, NP], U32, "xs_codes1")}
        xs_plane = [kept([P, NP], U8, "xs_plane%d" % a) for a in range(NGRP)]
        t_codes = [kept([P, NP], U32, "t_codes%d" % a) for a in range(NGRP)]
        t_plane = [kept([P, NP], U8, "t_plane%d" % a) for a in range(NGRP)]
        xs = []
        last = NSLICE - 1
        lin_tags = {XS_LOW_AFTER: "xs0", last: "xs1"}

        def new_entries(s, js):
            a, i = divmod(s, PACK)
            n = js.stop - js.start
            rows = slice(P * s, P * (s + 1))
            ang = psum.tile([P, n], F32, name="ang", tag=bank_tags[0])
            nc.tensor.matmul_mx(
                out=ang[:], lhsT=wb_codes[:, 2 * P * s : 2 * P * (s + 1)].bitcast(FP4X4), lhsT_scale=wb_plane[:, rows],
                rhs=v_codes[:, js].bitcast(FP8X4), rhs_scale=v_plane[:, js], start=True, stop=True,
            )
            turns = ring.tile([P, n], F32, name="turns")
            nc.scalar.activation(turns[:], ang[:], ACT.Copy, bias=0.25, scale=1.0 / (2.0 * math.pi))
            whole = ring.tile([P, n], U32, name="whole")
            nc.scalar.activation(whole[:], turns[:], ACT.Copy, bias=ROUNDER, scale=1.0)
            minus = ring.tile([P, n], F32, name="minus")
            nc.scalar.activation(minus[:], whole[:], ACT.Copy, bias=ROUNDER, scale=-1.0)
            frac = psum.tile([P, n], F32, name="frac", tag=bank_tags[1])
            add_transposed(frac, turns, minus, n)
            lin = psum.tile([P, n], F32, name="lin", tag=bank_tags[0] if js.start > 0 else bank_tags[2])
            for jt in range(n // P):
                cols = slice(js.start + P * jt, js.start + P * (jt + 1))
                nc.tensor.matmul_mx(
                    out=lin[:, P * jt : P * (jt + 1)], lhsT=v_codes[:, cols].bitcast(FP8X4), lhsT_scale=v_plane[:, cols],
                    rhs=wa_codes[:, rows].bitcast(FP8X4), rhs_scale=wa_plane[:, rows], start=True, stop=True,
                )
            cos_t = kept([P, n], F32, "cos_t", "xs_codes0") if s == last else ring.tile([P, n], F32, name="cos_t")
            nc.scalar.activation(cos_t[:], frac[:], ACT.Sin, scale=2.0 * math.pi)
            lin_t = kept([P, n], F32, "lin_t", lin_tags[s]) if s in lin_tags else ring.tile([P, n], F32, name="lin_t")
            nc.scalar.copy(lin_t[:], lin[:])
            total = psum.tile([P, n], F32, name="total", tag=bank_tags[3])
            add_transposed(total, cos_t, lin_t, n)
            h = ring.tile([P, n], F32, name="h", bufs=H_BUFS)
            nc.scalar.activation(h[:], total[:], ACT.Copy, scale=gain_t[:, a, i : i + 1])
            return h

        def put_entries(s, js, h):
            nc.vector.tensor_tensor(pages[s][:].indirect(entries(idx2, js)), h[:], wgs_t[:, s % PACK, js], ALU.mult)

        def fetch_x(s):
            a, i = divmod(s, PACK)
            nc.vector.tensor_copy(x[a][:, i, :], pages[s][:].indirect(idx3[:]))

        def scale_x(s):
            a, i = divmod(s, PACK)
            nc.scalar.activation(xs[a][:, i, :], x[a][:, i, :], ACT.Copy, scale=sc_t[:, a, i : i + 1])

        def fetch_whips(s):
            nc.vector.tensor_copy(whips[s // 2][:, s % 2, :], pages[s][:].indirect(idx4[:]))

        def prepare_w2(a, b):
            w2_woven = woven_weight_tile("w2_woven")
            for qs in (slice(0, P // 2), slice(P // 2, P)):
                dst, src = deal_and_weave_views(w2_raw[(a, b)], w2_woven, qs)
                nc.scalar.copy(dst, src)
            cols = slice(ROWS * b, ROWS * (b + 1))
            quantise(w2_codes[a][:, cols], w2_plane[a][:, cols], w2_woven[:])

        def walk(four_slices):
            return four_slices.rearrange("p i (c e) -> p c i e", e=RUN)

        def woven(flat):
            return flat.rearrange("p (c e i) -> p c i e", e=RUN, i=PACK)

        def weave_xs(a, jt):
            xs_woven = ring.tile([P, PACK * P], BF16, name="xs_woven", bufs=NGRP * JT, align_bytes=64)
            nc.scalar.copy(woven(xs_woven[:]), walk(xs[a][:, :, P * jt : P * (jt + 1)]))
            return xs_woven

        def quantise_xs(a, jt, xs_woven):
            cols = slice(P * jt, P * (jt + 1))
            quantise(xs_codes[a][:, cols], xs_plane[a][:, cols], xs_woven[:])

        w2_after = {2: w2_pieces[0:1], 3: w2_pieces[1:2], last: w2_pieces[2:]}
        for s in range(NSLICE):
            if s == last:
                xs.append(kept([P, PACK, NP], BF16, "xs0"))
                for low in range(PACK):
                    scale_x(low)
                xs_low_woven = [weave_xs(0, jt) for jt in range(JT)]
            for js in halves if s == 0 else [slice(0, S)]:
                h = new_entries(s, js)
                if s == last:
                    xs_codes[0] = kept([P, NP], U32, "xs_codes0")
                    for jt in range(JT):
                        quantise_xs(0, jt, xs_low_woven[jt])
                put_entries(s, js, h)
            fetch_x(s)
            if s < PACK:
                fetch_whips(s)
            for a, b in w2_after.get(s, []):
                prepare_w2(a, b)
        xs.append(kept([P, PACK, NP], BF16, "xs1"))
        whips.append(kept([P, 2, NP], F32, "whips2", "wgs_t"))
        for s in range(PACK, NSLICE):
            scale_x(s)

        pre_tanh = {}

        def second_stage_pass(jt, b, a):
            cols = slice(P * jt, P * (jt + 1))
            for i in range(PACK):
                rows = slice(ROWS * b + P * i, ROWS * b + P * (i + 1))
                nc.tensor.matmul_mx(
                    out=pre_tanh[(jt, b)][:, i, :], lhsT=w2_codes[a][:, rows].bitcast(FP8X4),
                    lhsT_scale=w2_plane[a][:, rows],
                    rhs=xs_codes[a][:, cols].bitcast(FP8X4), rhs_scale=xs_plane[a][:, cols],
                    start=(a == 0 and i == 0), stop=(a == NGRP - 1 and i == PACK - 1),
                )

        def gate_and_quantise(jt, b):
            cols = slice(P * jt, P * (jt + 1))
            gate = ring.tile([P, PACK * P], F32, name="gate", bufs=GATE_BUFS)
            gate_walk = gate[:].rearrange("p (c i e) -> p c i e", i=PACK, e=RUN)
            nc.scalar.activation(gate_walk, walk(pre_tanh[(jt, b)][:]), ACT.Tanh)
            t_woven = ring.tile([P, PACK * P], BF16, name="t_woven", bufs=T_BUFS, align_bytes=64)
            nc.vector.tensor_tensor(woven(t_woven[:]), gate_walk, walk(x[b][:, :, cols]), ALU.mult)
            quantise(t_codes[b][:, cols], t_plane[b][:, cols], t_woven[:])

        for jt in range(JT):
            for b in range(NGRP):
                tag = bank_tags[(NGRP * jt + b) % len(bank_tags)]
                pre_tanh[(jt, b)] = psum.tile([P, PACK, P], F32, name="pre_tanh", tag=tag)
                second_stage_pass(jt, b, 0)
        for jt in range(JT):
            quantise_xs(1, jt, weave_xs(1, jt))
        for jt in range(JT):
            for b in range(NGRP):
                second_stage_pass(jt, b, 1)
                gate_and_quantise(jt, b)
        whips.append(kept([P, 2, NP], F32, "whips3", "xs1"))
        for s in range(PACK, NSLICE):
            fetch_whips(s)

        w3_codes = kept([P, NGRP, H], I32, "w3_codes", "xs0")
        w3_plane = kept([P, H], U8, "w3_plane", "wa_plane")
        nc.vector.tensor_copy(
            w3_codes[:].rearrange("p a (b i q) -> p (a b) q i", b=NGRP, i=PACK),
            w3_raw[:].rearrange("p a (b q i) -> p (a b) q i", b=NGRP, i=PACK),
        )
        nc.vector.tensor_copy(
            w3_plane[:].rearrange("p (b i q) -> p b i q", b=NGRP, i=PACK),
            w3_plane_raw[:].rearrange("p (b q i) -> p b i q", b=NGRP, i=PACK),
        )
        for cols in halves:
            for pair in range(NSLICE // 2):
                slices = (2 * pair, 2 * pair + 1)
                b, i0 = divmod(slices[0], PACK)
                y = psum.tile([P, 2, NP // 2], F32, name="y", tag=bank_tags[pair])
                res = ring.tile([P, 2, NP // 2], F32, name="res", bufs=NSLICE)
                for a in range(NGRP):
                    for k, s in enumerate(slices):
                        rows = slice(P * s, P * (s + 1))
                        nc.tensor.matmul_mx(
                            out=y[:, k, :], lhsT=w3_codes[:, a, rows].bitcast(FP8X4),
                            lhsT_scale=w3_plane[PACK * a : P, rows],
                            rhs=t_codes[a][:, cols].bitcast(FP8X4), rhs_scale=t_plane[a][:, cols],
                            start=(a == 0 and k == 0), stop=(a == NGRP - 1 and k == 1),
                        )
                for k in range(2):
                    nc.vector.scalar_tensor_tensor(
                        res[:, k, :], whips[pair][:, k, cols], wv_t[:, b, i0 + k : i0 + k + 1], y[:, k, :],
                        ALU.mult, ALU.add,
                    )
                group = out[ROWS * b : ROWS * (b + 1), cols].rearrange("(p i) j -> p i j", i=PACK)
                nc.sync.dma_start(group[:, i0 : i0 + 2, :], res[:])
